import numpy as np
import ml_dtypes


def mxq(x, axis, fmt="e4m3"):
    dtype, down = {"e4m3": (ml_dtypes.float8_e4m3fn, 7), "e5m2": (ml_dtypes.float8_e5m2, 14)}[fmt]
    v = np.moveaxis(np.asarray(x, np.float32).astype(ml_dtypes.bfloat16).astype(np.float64), axis, -1)
    blocks = v.reshape(v.shape[:-1] + (-1, 32))
    amax = np.abs(blocks).max(-1, keepdims=True)
    byte = np.maximum(np.where(amax > 0, np.frexp(amax)[1] - 1 + 127, 0) - down, 1)
    scale = np.exp2(byte - 127.0)
    codes = (blocks / scale).astype(np.float32).astype(dtype).astype(np.float64)
    return np.moveaxis((codes * scale).reshape(v.shape), -1, axis)


WIDE = False


def mx_kscale(k):
    if not WIDE:
        return np.ones(k)
    levels = np.array([10, -10, 5, -5, 0])
    if k % 512:
        return np.exp2(np.random.permutation(np.resize(levels, k // 32))).repeat(32)
    a = np.empty((k // 512, 16))
    for p in range(k // 512):
        a[p, :8] = np.random.permutation(np.resize(levels, 8))
        for g in range(8):
            far = levels[np.abs(levels - a[p, g]) >= 10]
            a[p, g + 8] = far[np.random.randint(len(far))]
    return np.exp2(a.ravel()).repeat(32)


def f64(x):
    return np.asarray(x).astype(np.float64)


def striped(idx):
    return np.tile(idx.reshape(-1, 16).T, (8, 1)).astype(np.uint16)


def unstriped(offs):
    return offs[:16].T.reshape(-1).astype(np.int64)


E2M1 = np.array([0.0, 0.5, 1.0, 1.5, 2.0, 3.0, 4.0, 6.0, -0.0, -0.5, -1.0, -1.5, -2.0, -3.0, -4.0, -6.0])


def pack_weight(w, fmt):
    k, n = w.shape
    w = f64(np.asarray(w, np.float32).astype(ml_dtypes.bfloat16)).reshape(k // 32, 32, n)
    amax = np.abs(w).max(1)
    if fmt == "e4m3":
        byte = np.frexp(amax)[1] - 1 + 127 - 7
    else:
        mant, ex = np.frexp(amax / 6.0)
        byte = np.where(mant > 0.5, ex, ex - 1) + 127
    byte = np.clip(np.where(amax > 0, byte, 1), 1, 254)
    scaled = (w * np.exp2(127.0 - byte)[:, None, :]).reshape(k, n).astype(np.float32)
    by_word = np.ascontiguousarray(scaled.reshape(k // 512, 128, 4, n).transpose(0, 1, 3, 2))
    if fmt == "e4m3":
        words = by_word.astype(ml_dtypes.float8_e4m3fn).view(np.uint8)
    else:
        c = by_word.astype(ml_dtypes.float4_e2m1fn).view(np.uint8) & 0xF
        words = (c[..., 0::2] | (c[..., 1::2] << 4)).reshape(k // 512, 128, 2 * n)
    return np.ascontiguousarray(words), np.ascontiguousarray(byte.astype(np.uint8).reshape(k // 512, 16, n))


def unpack_weight(words, scales, fmt):
    g, _, n = scales.shape
    words = np.ascontiguousarray(words).reshape(g, 128, n, -1)
    if fmt == "e4m3":
        vals = words.view(ml_dtypes.float8_e4m3fn).astype(np.float64)
    else:
        nib = np.empty((g, 128, n, 4), np.uint8)
        nib[..., 0::2] = words & 0xF
        nib[..., 1::2] = words >> 4
        vals = E2M1[nib]
    vals = vals * np.repeat(np.exp2(scales.astype(np.float64) - 127.0), 8, axis=1)[..., None]
    return vals.transpose(0, 1, 3, 2).reshape(g * 512, n)


def gelu(v):
    return 0.5 * v * (1.0 + np.tanh(np.sqrt(2.0 / np.pi) * (v + 0.044715 * v**3)))


K, K2, H, N, T, S = 1024, 512, 1024, 512, 2048, 1024


def setup_inputs():
    n = np.random.standard_normal
    s = mx_kscale(K)[:, None]
    s2 = mx_kscale(K2)[:, None]
    u = mx_kscale(H)[:, None]
    d = {}
    d["tab_words"], d["tab_scales"] = pack_weight(n((K, T)) * s, "e4m3")
    d["offs"] = striped(np.random.permutation(T)[:S])
    d["w1"] = (n((K, H)) / s / K ** 0.5).astype(np.float32)
    d["xs_words"], d["xs_scales"] = pack_weight(n((K2, S)) * s2, "e4m3")
    d["wx_words"], d["wx_scales"] = pack_weight(n((K2, H)) / s2 / K2 ** 0.5, "e2m1")
    d["gain1"] = (np.exp(0.3 * n(H)) * u[:, 0]).astype(np.float32)
    d["gain2"] = (np.exp(0.3 * n(H)) * u[:, 0]).astype(np.float32)
    d["w3"] = (n((H, N)) / u / H ** 0.5).astype(np.float32)
    d["w4_words"], d["w4_scales"] = pack_weight(n((H, N)) / u / H ** 0.5, "e2m1")
    return d


def reference(tab_words, tab_scales, offs, w1, xs_words, xs_scales, wx_words, wx_scales,
              gain1, gain2, w3, w4_words, w4_scales):
    v = unpack_weight(tab_words, tab_scales, "e4m3")[:, unstriped(offs)]
    xs = unpack_weight(xs_words, xs_scales, "e4m3")
    wx = unpack_weight(wx_words, wx_scales, "e2m1")
    w4 = unpack_weight(w4_words, w4_scales, "e2m1")
    w1q = mxq(f64(w1), 0, "e4m3")
    w3q = mxq(f64(w3), 0, "e4m3")
    load = w1q.T @ v + wx.T @ xs
    a = load / (1.0 + np.exp(-load)) * f64(gain1)[:, None]
    b = np.abs(load) * f64(gain2)[:, None]
    aq = mxq(a, 0, "e4m3")
    bq = mxq(b, 0, "e4m3")
    out = (w3q.T @ aq) - (w4.T @ bq)
    return out

@@ -1,0 +1,315 @@
+from contextlib import ExitStack
+
+import concourse.mybir as mybir
+
+K, K2, H, N, T, S = 1024, 512, 1024, 512, 2048, 1024
+FLOPS = 2 * S * (K * H + K2 * H + 2 * H * N)
+
+F32 = mybir.dt.float32
+BF16 = mybir.dt.bfloat16
+I32 = mybir.dt.int32
+U32 = mybir.dt.uint32
+U16 = mybir.dt.uint16
+U8 = mybir.dt.uint8
+E4M3 = mybir.dt.float8_e4m3fn_x4
+E2M1 = mybir.dt.float4_e2m1fn_x4
+ACT = mybir.ActivationFunctionType
+ALU = mybir.AluOpType
+
+P = 128
+PACK = 4
+PASS = P * PACK
+HALF = 512
+QUADS = 4
+
+
+def tile_list_laundry_dosing_scores_kernel(
+    tc, tab_words, tab_scales, offs, w1, xs_words, xs_scales, wx_words, wx_scales,
+    gain1, gain2, w3, w4_words, w4_scales, out,
+):
+    nc = tc.nc
+    with ExitStack() as ctx:
+        keep = ctx.enter_context(tc.tile_pool(name="keep", bufs=1))
+        work = ctx.enter_context(tc.tile_pool(name="work", bufs=2))
+        psum = ctx.enter_context(tc.psum_pool(name="psum", bufs=8))
+
+        def held(name, shape, dtype):
+            return keep.tile(shape, dtype, name=name, align_bytes=64)
+
+        offsets = keep.tile([P, S // 16], U16, name="offsets")
+        nc.sync.dma_start(offsets[:], offs)
+
+        warm_in = held("warm_in", [P, 8], F32)
+        warm_out = held("warm_out", [P, 8], F32)
+        nc.vector.memset(warm_in[:], 0.0)
+        nc.scalar.activation(warm_out[:], warm_in[:], ACT.Silu)
+
+        tab_sc = held("tab_sc", [P, T], U8)
+        wx_sc_raw = held("wx_sc_raw", [P, H], U8)
+        xs_sc = held("xs_sc", [P, S], U8)
+        w4_sc = held("w4_sc", [P, 2, N], U8)
+        nc.gpsimd.memset(tab_sc[:].bitcast(I32), 0)
+        nc.gpsimd.memset(wx_sc_raw[:].bitcast(I32), 0)
+        nc.gpsimd.memset(xs_sc[:].bitcast(I32), 0)
+        nc.gpsimd.memset(w4_sc[:].bitcast(I32), 0)
+
+        wx_raw = [held("wx_raw%d" % b, [P, 2 * PASS], U8) for b in range(2)]
+        xs = [held("xs%d" % h, [P, HALF], I32) for h in range(2)]
+
+        def load_wx(b):
+            nc.sync.dma_start(wx_raw[b][:].bitcast(I32), wx_words[0, :, 2 * PASS * b : 2 * PASS * (b + 1)].bitcast(I32))
+
+        def load_xs(h):
+            nc.sync.dma_start(xs[h][:], xs_words[0].rearrange("p n i -> p (n i)").bitcast(I32)[:, HALF * h : HALF * (h + 1)])
+
+        load_wx(0)
+
+        tab = [held("tab%d" % a, [P, T], I32) for a in range(2)]
+
+        def load_tab(a):
+            nc.sync.dma_start(tab[a][:], tab_words[a].rearrange("p n i -> p (n i)").bitcast(I32))
+
+        def load_w(name, rows):
+            raw = held(name, [P, PACK, rows.shape[1]], F32)
+            nc.sync.dma_start(raw[:], rows.rearrange("(p i) c -> p i c", i=PACK))
+            return raw
+
+        def w1_rows(a, b):
+            return w1[PASS * a : PASS * (a + 1), PASS * b : PASS * (b + 1)]
+
+        load_tab(0)
+        for q in range(QUADS):
+            nc.sync.dma_start(tab_sc[32 * q : 32 * q + 8, :].bitcast(I32), tab_scales[:, 4 * q : 4 * q + 4, :].bitcast(I32))
+        w1_raw = {}
+        w1_raw[0, 0] = load_w("w1_raw00", w1_rows(0, 0))
+        for q in range(QUADS):
+            nc.sync.dma_start(wx_sc_raw[32 * q : 32 * q + 4, :].bitcast(I32), wx_scales[0, 4 * q : 4 * q + 4, :].bitcast(I32))
+        load_tab(1)
+        w1_last = [load_w(name, w1_rows(1, 0)[:, 256 * e : 256 * (e + 1)]) for e, name in enumerate(["w1_raw100", "first_then_v_sc1"])]
+        for q in range(QUADS):
+            nc.sync.dma_start(xs_sc[32 * q : 32 * q + 4, :].bitcast(I32), xs_scales[0, 4 * q : 4 * q + 4, :].bitcast(I32))
+        load_xs(0)
+        g1 = held("g1", [P, 2, PACK], F32)
+        g2 = held("g2", [P, 2, PACK], F32)
+        nc.sync.dma_start(g1[:], gain1.rearrange("(b p t) -> p b t", b=2, t=PACK))
+        nc.sync.dma_start(g2[:], gain2.rearrange("(b p t) -> p b t", b=2, t=PACK))
+        load_xs(1)
+        load_wx(1)
+        w1_raw[0, 1] = load_w("w1_raw01", w1_rows(0, 1))
+        w1_raw[1, 1] = load_w("w1_raw11", w1_rows(1, 1))
+        w3_raw = [load_w("w3_raw%d" % b, w3[PASS * b : PASS * (b + 1), :]) for b in range(2)]
+        w4 = held("w4", [P, 2, 2 * N], U8)
+        nc.sync.dma_start(w4[:].bitcast(I32), w4_words.rearrange("b p n -> p b n").bitcast(I32))
+        for q in range(QUADS):
+            nc.sync.dma_start(
+                w4_sc[32 * q : 32 * q + 4, :, :].bitcast(I32),
+                w4_scales[:, 4 * q : 4 * q + 4, :].rearrange("b r n -> r b n").bitcast(I32),
+            )
+
+        wx = held("wx", [P, 2 * H], U8)
+        wx_sc = {}
+
+        def deal_wx_words(b):
+            nc.vector.tensor_copy(
+                wx[:, 2 * PASS * b : 2 * PASS * (b + 1)].bitcast(U16).rearrange("p (t m) -> p m t", t=PACK),
+                wx_raw[b][:].bitcast(U16).rearrange("p (m t) -> p m t", t=PACK),
+            )
+
+        deal_wx_words(0)
+
+        def deal_wx_scales(b, tag):
+            cols = slice(PASS * b, PASS * (b + 1))
+            wx_sc[b] = keep.tile([P, PASS], U8, name="wx_sc%d" % b, tag=tag, align_bytes=64)
+            nc.vector.tensor_copy(
+                wx_sc[b][:].rearrange("p (t m) -> p m t", t=PACK),
+                wx_sc_raw[:, cols].rearrange("p (m t) -> p m t", t=PACK),
+            )
+
+        v = {}
+        v_sc = {}
+
+        def picks(h):
+            return offsets[:, (HALF // 16) * h : (HALF // 16) * (h + 1)]
+
+        def gather_words(a, h, tag):
+            v[a, h] = keep.tile([P, HALF], U32, name="v%d%d" % (a, h), tag=tag, align_bytes=64)
+            nc.vector.tensor_copy(v[a, h][:], tab[a][:].bitcast(U32).indirect(picks(h)))
+
+        def gather_scales(h, tag):
+            v_sc[h] = keep.tile([P, HALF], U8, name="v_sc%d" % h, tag=tag, align_bytes=64)
+            nc.vector.tensor_copy(v_sc[h][:], tab_sc[:].indirect(picks(h)))
+
+        def copy_on(engine, dst, src):
+            if engine == "scalar":
+                nc.scalar.copy(dst, src)
+            else:
+                nc.vector.tensor_copy(dst, src)
+
+        def quantize(name, grouped):
+            codes = held(name, [P, PASS], U32)
+            scales = held(name + "_sc", [P, PASS], U8)
+            nc.vector.quantize_mx(codes[:].bitcast(E4M3), scales[:], grouped[:])
+            return codes, scales
+
+        def round_w1(a, b, engine):
+            grouped = work.tile([P, PACK * PASS], BF16, name="w_grouped", align_bytes=64)
+            copy_on(
+                engine,
+                grouped[:].rearrange("p (t m i) -> p m i t", t=PACK, i=PACK),
+                w1_raw[a, b][:].rearrange("p i (m t) -> p m i t", t=PACK),
+            )
+            return grouped
+
+        def round_w3(b, engine):
+            grouped = work.tile([P, PACK * PASS], BF16, name="w_grouped", align_bytes=64)
+            copy_on(
+                engine,
+                grouped[:].rearrange("p (c n i) -> p c i n", n=4, i=PACK),
+                w3_raw[b][:].rearrange("p i (c n) -> p c i n", n=4),
+            )
+            return grouped
+
+        w1q = {}
+        gather_words(0, 0, "v00")
+        gather_scales(0, "v_sc0")
+        deal_wx_scales(0, "wx_sc0")
+        w1q[0, 0] = quantize("w1q00", round_w1(0, 0, "scalar"))
+        gather_words(1, 0, "v10")
+        grouped10 = keep.tile([P, PACK * PASS], BF16, name="grouped10", tag="first_then_v11", align_bytes=64)
+        for e, engine in enumerate(["scalar", "vector"]):
+            copy_on(
+                engine,
+                grouped10[:].rearrange("p (t m i) -> p m i t", t=PACK, i=PACK)[:, 64 * e : 64 * (e + 1)],
+                w1_last[e][:].rearrange("p i (m t) -> p m i t", t=PACK),
+            )
+        w1q[1, 0] = quantize("w1q10", grouped10)
+
+        below = held("below", [P, 2, PACK], F32)
+        flip = held("flip", [P, 2, PACK], F32)
+        nc.vector.tensor_scalar(below[:], g2[:], 0.0, 2.0, ALU.is_lt, ALU.mult)
+        nc.vector.tensor_scalar(flip[:], below[:], -1.0, None, ALU.add)
+
+        def first_stage(b, h):
+            banks = [psum.tile([P, HALF], F32, name="bank") for t in range(PACK)]
+            cols = slice(HALF * h, HALF * (h + 1))
+
+            def table_pass(a, t):
+                codes, scales = w1q[a, b]
+                m = slice(P * t, P * (t + 1))
+                nc.tensor.matmul_mx(
+                    banks[t][:], lhsT=codes[:, m].bitcast(E4M3), lhsT_scale=scales[:, m],
+                    rhs=v[a, h][:].bitcast(E4M3), rhs_scale=v_sc[h][4 * a : P, :],
+                    start=(a == 0), stop=False,
+                )
+
+            for t in range(PACK):
+                table_pass(0, t)
+            for t in range(PACK):
+                table_pass(1, t)
+                c0 = PASS * b + P * t
+                nc.tensor.matmul_mx(
+                    banks[t][:], lhsT=wx[:, 2 * c0 : 2 * (c0 + P)].bitcast(E2M1), lhsT_scale=wx_sc[b][:, P * t : P * (t + 1)],
+                    rhs=xs[h][:].bitcast(E4M3), rhs_scale=xs_sc[:, cols],
+                    start=False, stop=True,
+                )
+            return banks
+
+        def interleave(name, planes, width):
+            grouped = work.tile([P, PACK * width], BF16, name=name, align_bytes=64)
+            nc.vector.tensor_copy(
+                grouped[:].rearrange("p (c i t) -> p c t i", i=4, t=PACK),
+                planes[:].rearrange("p t (c i) -> p c t i", i=4),
+            )
+            return grouped
+
+        def operand(name):
+            return held(name, [P, HALF], U32), held(name + "_sc", [P, HALF], U8)
+
+        aq = {(b, h): operand("aq%d%d" % (b, h)) for b in range(2) for h in range(2)}
+        bq = {(b, h): operand("bq%d%d" % (b, h)) for b in range(2) for h in range(2)}
+
+        def responses(b, h, banks, c0, width):
+            cols = slice(c0, c0 + width)
+            a_planes = work.tile([P, PACK, width], BF16, name="a_planes", align_bytes=64)
+            b_planes = work.tile([P, PACK, width], BF16, name="b_planes", align_bytes=64)
+            for t in range(PACK):
+                silu = work.tile([P, width], F32, name="silu", bufs=6)
+                nc.scalar.activation(silu[:], banks[t][:, cols], ACT.Silu)
+                nc.vector.tensor_scalar(a_planes[:, t, :], silu[:], g1[:, b, t : t + 1], None, ALU.mult)
+            a_grouped = interleave("a_grouped", a_planes, width)
+            for t in range(PACK):
+                size = work.tile([P, width], BF16, name="size", bufs=6)
+                nc.scalar.activation(size[:], banks[t][:, cols], ACT.Abs, scale=g2[:, b, t : t + 1])
+                nc.vector.tensor_scalar(b_planes[:, t, :], size[:], flip[:, b, t : t + 1], None, ALU.mult)
+            nc.vector.quantize_mx(aq[b, h][0][:, cols].bitcast(E4M3), aq[b, h][1][:, cols], a_grouped[:])
+            b_grouped = interleave("b_grouped", b_planes, width)
+            nc.vector.quantize_mx(bq[b, h][0][:, cols].bitcast(E4M3), bq[b, h][1][:, cols], b_grouped[:])
+
+        w3q = {}
+
+        def open_sums(width):
+            per_bank = HALF // width
+            return [psum.tile([P, per_bank, width], F32, name="bank") for k in range(N // P // per_bank)]
+
+        def second_stage(sums, b, h, c0, width):
+            per_bank = HALF // width
+            narrow = HALF if width == HALF else P
+            codes, scales = w3q[b]
+            cols = slice(c0, c0 + width)
+            for u in range(N // P):
+                m = slice(P * u, P * (u + 1))
+                nc.tensor.matmul_mx(
+                    sums[u // per_bank][:, u % per_bank, :], lhsT=codes[:, m].bitcast(E4M3), lhsT_scale=scales[:, m],
+                    rhs=aq[b, h][0][:, cols].bitcast(E4M3), rhs_scale=aq[b, h][1][:, cols],
+                    start=(b == 0 and u % per_bank == 0), stop=False,
+                )
+            for u in range(N // P):
+                for d in range(0, width, narrow):
+                    part = slice(c0 + d, c0 + d + narrow)
+                    nc.tensor.matmul_mx(
+                        sums[u // per_bank][:, u % per_bank, d : d + narrow],
+                        lhsT=w4[:, b, 2 * P * u : 2 * P * (u + 1)].bitcast(E2M1),
+                        lhsT_scale=w4_sc[:, b, P * u : P * (u + 1)],
+                        rhs=bq[b, h][0][:, part].bitcast(E4M3), rhs_scale=bq[b, h][1][:, part],
+                        start=False, stop=(b == 1 and u % per_bank == per_bank - 1 and d + narrow == width),
+                    )
+
+        def store(sums, j0, width, engines):
+            per_bank = HALF // width
+            for k, bank in enumerate(sums):
+                result = work.tile([P, per_bank, width], F32, name="result", bufs=8)
+                copy_on(engines[k], result[:], bank[:])
+                rows = out[P * per_bank * k : P * per_bank * (k + 1), j0 : j0 + width]
+                nc.sync.dma_start(rows.rearrange("(u p) c -> p u c", p=P), result[:])
+
+        banks00 = first_stage(0, 0)
+        gather_words(0, 1, "v01")
+        gather_scales(1, "first_then_v_sc1")
+        gather_words(1, 1, "first_then_v11")
+        banks01 = first_stage(0, 1)
+        responses(0, 0, banks00, 0, HALF)
+        deal_wx_words(1)
+        deal_wx_scales(1, "w1_raw100")
+        w1q[0, 1] = quantize("w1q01", round_w1(0, 1, "scalar"))
+        w1q[1, 1] = quantize("w1q11", round_w1(1, 1, "vector"))
+        banks10 = first_stage(1, 0)
+        responses(0, 1, banks01, 0, HALF)
+        w3q[0] = quantize("w3q0", round_w3(0, "scalar"))
+        sums0 = open_sums(HALF)
+        second_stage(sums0, 0, 0, 0, HALF)
+        responses(1, 0, banks10, 0, HALF)
+        banks11 = first_stage(1, 1)
+        w3q[1] = quantize("w3q1", round_w3(1, "scalar"))
+        second_stage(sums0, 1, 0, 0, HALF)
+        chunks = [(0, 256), (256, 256)]
+        responses(1, 1, banks11, chunks[0][0], chunks[0][1])
+        store(sums0, 0, HALF, ["scalar", "vector"] * 2)
+        sums1 = [open_sums(width) for c0, width in chunks]
+        for sums, (c0, width) in zip(sums1, chunks):
+            second_stage(sums, 0, 1, c0, width)
+        for k, (c0, width) in enumerate(chunks):
+            if k > 0:
+                responses(1, 1, banks11, c0, width)
+                store(sums1[k - 1], HALF + chunks[k - 1][0], chunks[k - 1][1], ["scalar", "scalar"])
+            second_stage(sums1[k], 1, 1, c0, width)
+        store(sums1[-1], HALF + chunks[-1][0], chunks[-1][1], ["scalar", "vector"])

@@ -21,6 +21,7 @@ PACK = 4
 PASS = P * PACK
 HALF = 512
 QUADS = 4
+STEP = 256
 
 
 def tile_list_laundry_dosing_scores_kernel(
@@ -84,8 +85,8 @@ def tile_list_laundry_dosing_scores_kernel(
         w1_raw[0, 0] = load_w("w1_raw00", w1_rows(0, 0))
         for q in range(QUADS):
             nc.sync.dma_start(wx_sc_raw[32 * q : 32 * q + 4, :].bitcast(I32), wx_scales[0, 4 * q : 4 * q + 4, :].bitcast(I32))
+        w1_raw[1, 0] = load_w("w1_raw10", w1_rows(1, 0))
         load_tab(1)
-        w1_last = [load_w(name, w1_rows(1, 0)[:, 256 * e : 256 * (e + 1)]) for e, name in enumerate(["w1_raw100", "first_then_v_sc1"])]
         for q in range(QUADS):
             nc.sync.dma_start(xs_sc[32 * q : 32 * q + 4, :].bitcast(I32), xs_scales[0, 4 * q : 4 * q + 4, :].bitcast(I32))
         load_xs(0)
@@ -151,8 +152,8 @@ def tile_list_laundry_dosing_scores_kernel(
             nc.vector.quantize_mx(codes[:].bitcast(E4M3), scales[:], grouped[:])
             return codes, scales
 
-        def round_w1(a, b, engine):
-            grouped = work.tile([P, PACK * PASS], BF16, name="w_grouped", align_bytes=64)
+        def round_w1(a, b, engine, tag):
+            grouped = keep.tile([P, PACK * PASS], BF16, name="w1_grouped%d%d" % (a, b), tag=tag, align_bytes=64)
             copy_on(
                 engine,
                 grouped[:].rearrange("p (t m i) -> p m i t", t=PACK, i=PACK),
@@ -173,54 +174,50 @@ def tile_list_laundry_dosing_scores_kernel(
         gather_words(0, 0, "v00")
         gather_scales(0, "v_sc0")
         deal_wx_scales(0, "wx_sc0")
-        w1q[0, 0] = quantize("w1q00", round_w1(0, 0, "scalar"))
-        gather_words(1, 0, "v10")
-        grouped10 = keep.tile([P, PACK * PASS], BF16, name="grouped10", tag="first_then_v11", align_bytes=64)
-        for e, engine in enumerate(["scalar", "vector"]):
-            copy_on(
-                engine,
-                grouped10[:].rearrange("p (t m i) -> p m i t", t=PACK, i=PACK)[:, 64 * e : 64 * (e + 1)],
-                w1_last[e][:].rearrange("p i (m t) -> p m i t", t=PACK),
+        w1q[0, 0] = quantize("w1q00", round_w1(0, 0, "scalar", "v_sc1"))
+        codes10 = held("w1q10", [P, PASS], U32)
+        scales10 = held("w1q10_sc", [P, PASS], U8)
+        for e in range(2):
+            grouped = keep.tile([P, 2 * PASS], BF16, name="w1_half%d" % e, tag=["w1_half0", "wx_sc1"][e], align_bytes=64)
+            nc.scalar.copy(
+                grouped[:].rearrange("p (t m i) -> p m i t", t=2, i=PACK),
+                w1_raw[1, 0][:].rearrange("p i (m t) -> p m i t", t=PACK)[:, :, :, 2 * e : 2 * e + 2],
             )
-        w1q[1, 0] = quantize("w1q10", grouped10)
+            cols = slice(256 * e, 256 * (e + 1))
+            nc.vector.quantize_mx(codes10[:, cols].bitcast(E4M3), scales10[:, cols], grouped[:])
+        w1q[1, 0] = codes10, scales10
+        gather_words(1, 0, "v10")
 
-        below = held("below", [P, 2, PACK], F32)
-        flip = held("flip", [P, 2, PACK], F32)
-        nc.vector.tensor_scalar(below[:], g2[:], 0.0, 2.0, ALU.is_lt, ALU.mult)
-        nc.vector.tensor_scalar(flip[:], below[:], -1.0, None, ALU.add)
+        gains = held("gains", [P, 2, 2, PACK], F32)
+        nc.vector.tensor_copy(gains[:, :, 0, :], g1[:])
+        nc.vector.tensor_scalar(gains[:, :, 1, :], g2[:], -1.0, None, ALU.mult)
 
         def first_stage(b, h):
-            banks = [psum.tile([P, HALF], F32, name="bank") for t in range(PACK)]
-            cols = slice(HALF * h, HALF * (h + 1))
+            banks = [psum.tile([P, PACK, P], F32, name="bank") for c in range(PACK)]
 
-            def table_pass(a, t):
+            def table_pass(a, c):
                 codes, scales = w1q[a, b]
-                m = slice(P * t, P * (t + 1))
-                nc.tensor.matmul_mx(
-                    banks[t][:], lhsT=codes[:, m].bitcast(E4M3), lhsT_scale=scales[:, m],
-                    rhs=v[a, h][:].bitcast(E4M3), rhs_scale=v_sc[h][4 * a : P, :],
-                    start=(a == 0), stop=False,
-                )
+                cols = slice(P * c, P * (c + 1))
+                for t in range(PACK):
+                    m = slice(P * t, P * (t + 1))
+                    nc.tensor.matmul_mx(
+                        banks[c][:, t, :], lhsT=codes[:, m].bitcast(E4M3), lhsT_scale=scales[:, m],
+                        rhs=v[a, h][:, cols].bitcast(E4M3), rhs_scale=v_sc[h][4 * a : P, cols],
+                        start=(a == 0 and t == 0), stop=(a == 1 and t == PACK - 1),
+                    )
 
-            for t in range(PACK):
-                table_pass(0, t)
-            for t in range(PACK):
-                table_pass(1, t)
-                c0 = PASS * b + P * t
-                nc.tensor.matmul_mx(
-                    banks[t][:], lhsT=wx[:, 2 * c0 : 2 * (c0 + P)].bitcast(E2M1), lhsT_scale=wx_sc[b][:, P * t : P * (t + 1)],
-                    rhs=xs[h][:].bitcast(E4M3), rhs_scale=xs_sc[:, cols],
-                    start=False, stop=True,
-                )
+            for c in range(PACK):
+                table_pass(0, c)
+            for c in range(PACK):
+                for t in range(PACK):
+                    c0 = PASS * b + P * t
+                    nc.tensor.matmul_mx(
+                        banks[c][:, t, :], lhsT=wx[:, 2 * c0 : 2 * (c0 + P)].bitcast(E2M1), lhsT_scale=wx_sc[b][:, P * t : P * (t + 1)],
+                        rhs=xs[h][:, P * c : P * (c + 1)].bitcast(E4M3), rhs_scale=xs_sc[:, HALF * h + P * c : HALF * h + P * (c + 1)],
+                        start=False, stop=False,
+                    )
+                table_pass(1, c)
             return banks
-
-        def interleave(name, planes, width):
-            grouped = work.tile([P, PACK * width], BF16, name=name, align_bytes=64)
-            nc.vector.tensor_copy(
-                grouped[:].rearrange("p (c i t) -> p c t i", i=4, t=PACK),
-                planes[:].rearrange("p t (c i) -> p c t i", i=4),
-            )
-            return grouped
 
         def operand(name):
             return held(name, [P, HALF], U32), held(name + "_sc", [P, HALF], U8)
@@ -229,21 +226,21 @@ def tile_list_laundry_dosing_scores_kernel(
         bq = {(b, h): operand("bq%d%d" % (b, h)) for b in range(2) for h in range(2)}
 
         def responses(b, h, banks, c0, width):
-            cols = slice(c0, c0 + width)
-            a_planes = work.tile([P, PACK, width], BF16, name="a_planes", align_bytes=64)
-            b_planes = work.tile([P, PACK, width], BF16, name="b_planes", align_bytes=64)
-            for t in range(PACK):
-                silu = work.tile([P, width], F32, name="silu", bufs=6)
-                nc.scalar.activation(silu[:], banks[t][:, cols], ACT.Silu)
-                nc.vector.tensor_scalar(a_planes[:, t, :], silu[:], g1[:, b, t : t + 1], None, ALU.mult)
-            a_grouped = interleave("a_grouped", a_planes, width)
-            for t in range(PACK):
-                size = work.tile([P, width], BF16, name="size", bufs=6)
-                nc.scalar.activation(size[:], banks[t][:, cols], ACT.Abs, scale=g2[:, b, t : t + 1])
-                nc.vector.tensor_scalar(b_planes[:, t, :], size[:], flip[:, b, t : t + 1], None, ALU.mult)
-            nc.vector.quantize_mx(aq[b, h][0][:, cols].bitcast(E4M3), aq[b, h][1][:, cols], a_grouped[:])
-            b_grouped = interleave("b_grouped", b_planes, width)
-            nc.vector.quantize_mx(bq[b, h][0][:, cols].bitcast(E4M3), bq[b, h][1][:, cols], b_grouped[:])
+            for d in range(c0, c0 + width, STEP):
+                step = min(STEP, width)
+                grouped = work.tile([P, 2, step // P, PASS], BF16, name="grouped", bufs=3, align_bytes=64)
+                for k in range(step // P):
+                    both = work.tile([P, 2, P, PACK], F32, name="both", bufs=5)
+                    sums = banks[d // P + k][:].rearrange("p t c -> p c t")
+                    nc.scalar.activation(both[:, 0], sums, ACT.Silu)
+                    nc.scalar.activation(both[:, 1], sums, ACT.Abs)
+                    nc.vector.tensor_tensor(
+                        grouped[:, :, k, :].rearrange("p e (c t) -> p e c t", t=PACK), both[:],
+                        gains[:, b].unsqueeze(2).broadcast_to([P, 2, P, PACK]), ALU.mult,
+                    )
+                cols = slice(d, d + step)
+                for e, (codes, scales) in enumerate((aq[b, h], bq[b, h])):
+                    nc.vector.quantize_mx(codes[:, cols].bitcast(E4M3), scales[:, cols], grouped[:, e].rearrange("p k c -> p (k c)"))
 
         w3q = {}
 
@@ -284,14 +281,14 @@ def tile_list_laundry_dosing_scores_kernel(
 
         banks00 = first_stage(0, 0)
         gather_words(0, 1, "v01")
-        gather_scales(1, "first_then_v_sc1")
-        gather_words(1, 1, "first_then_v11")
+        gather_scales(1, "v_sc1")
+        gather_words(1, 1, "v11")
         banks01 = first_stage(0, 1)
         responses(0, 0, banks00, 0, HALF)
         deal_wx_words(1)
-        deal_wx_scales(1, "w1_raw100")
-        w1q[0, 1] = quantize("w1q01", round_w1(0, 1, "scalar"))
-        w1q[1, 1] = quantize("w1q11", round_w1(1, 1, "vector"))
+        deal_wx_scales(1, "wx_sc1")
+        w1q[0, 1] = quantize("w1q01", round_w1(0, 1, "scalar", "w1_grouped01"))
+        w1q[1, 1] = quantize("w1q11", round_w1(1, 1, "vector", "w1_grouped11"))
         banks10 = first_stage(1, 0)
         responses(0, 1, banks01, 0, HALF)
         w3q[0] = quantize("w3q0", round_w3(0, "scalar"))
@@ -301,9 +298,9 @@ def tile_list_laundry_dosing_scores_kernel(
         banks11 = first_stage(1, 1)
         w3q[1] = quantize("w3q1", round_w3(1, "scalar"))
         second_stage(sums0, 1, 0, 0, HALF)
-        chunks = [(0, 256), (256, 256)]
+        chunks = [(0, 128), (128, 128), (256, 128), (384, 128)]
         responses(1, 1, banks11, chunks[0][0], chunks[0][1])
-        store(sums0, 0, HALF, ["scalar", "vector"] * 2)
+        store(sums0, 0, HALF, ["scalar"] * 4)
         sums1 = [open_sums(width) for c0, width in chunks]
         for sums, (c0, width) in zip(sums1, chunks):
             second_stage(sums, 0, 1, c0, width)

@@ -32,7 +32,7 @@ def tile_list_laundry_dosing_scores_kernel(
     with ExitStack() as ctx:
         keep = ctx.enter_context(tc.tile_pool(name="keep", bufs=1))
         work = ctx.enter_context(tc.tile_pool(name="work", bufs=2))
-        psum = ctx.enter_context(tc.psum_pool(name="psum", bufs=8))
+        psum = ctx.enter_context(tc.psum_pool(name="psum", bufs=1))
 
         def held(name, shape, dtype):
             return keep.tile(shape, dtype, name=name, align_bytes=64)
@@ -54,16 +54,13 @@ def tile_list_laundry_dosing_scores_kernel(
         nc.gpsimd.memset(xs_sc[:].bitcast(I32), 0)
         nc.gpsimd.memset(w4_sc[:].bitcast(I32), 0)
 
-        wx_raw = [held("wx_raw%d" % b, [P, 2 * PASS], U8) for b in range(2)]
+        wx_raw = held("wx_raw", [P, 2 * H], U8)
         xs = [held("xs%d" % h, [P, HALF], I32) for h in range(2)]
-
-        def load_wx(b):
-            nc.sync.dma_start(wx_raw[b][:].bitcast(I32), wx_words[0, :, 2 * PASS * b : 2 * PASS * (b + 1)].bitcast(I32))
 
         def load_xs(h):
             nc.sync.dma_start(xs[h][:], xs_words[0].rearrange("p n i -> p (n i)").bitcast(I32)[:, HALF * h : HALF * (h + 1)])
 
-        load_wx(0)
+        nc.sync.dma_start(wx_raw[:].bitcast(I32), wx_words[0].bitcast(I32))
 
         tab = [held("tab%d" % a, [P, T], I32) for a in range(2)]
 
@@ -95,7 +92,6 @@ def tile_list_laundry_dosing_scores_kernel(
         nc.sync.dma_start(g1[:], gain1.rearrange("(b p t) -> p b t", b=2, t=PACK))
         nc.sync.dma_start(g2[:], gain2.rearrange("(b p t) -> p b t", b=2, t=PACK))
         load_xs(1)
-        load_wx(1)
         w1_raw[0, 1] = load_w("w1_raw01", w1_rows(0, 1))
         w1_raw[1, 1] = load_w("w1_raw11", w1_rows(1, 1))
         w3_raw = [load_w("w3_raw%d" % b, w3[PASS * b : PASS * (b + 1), :]) for b in range(2)]
@@ -108,21 +104,16 @@ def tile_list_laundry_dosing_scores_kernel(
             )
 
         wx = held("wx", [P, 2 * H], U8)
-        wx_sc = {}
+        wx_sc = held("wx_sc", [P, H], U8)
+        nc.vector.tensor_copy(
+            wx[:].bitcast(U16).rearrange("p (b t m) -> p b m t", b=2, t=PACK),
+            wx_raw[:].bitcast(U16).rearrange("p (b m t) -> p b m t", b=2, t=PACK),
+        )
 
-        def deal_wx_words(b):
-            nc.vector.tensor_copy(
-                wx[:, 2 * PASS * b : 2 * PASS * (b + 1)].bitcast(U16).rearrange("p (t m) -> p m t", t=PACK),
-                wx_raw[b][:].bitcast(U16).rearrange("p (m t) -> p m t", t=PACK),
-            )
-
-        deal_wx_words(0)
-
-        def deal_wx_scales(b, tag):
+        def deal_wx_scales(b):
             cols = slice(PASS * b, PASS * (b + 1))
-            wx_sc[b] = keep.tile([P, PASS], U8, name="wx_sc%d" % b, tag=tag, align_bytes=64)
             nc.vector.tensor_copy(
-                wx_sc[b][:].rearrange("p (t m) -> p m t", t=PACK),
+                wx_sc[:, cols].rearrange("p (t m) -> p m t", t=PACK),
                 wx_sc_raw[:, cols].rearrange("p (m t) -> p m t", t=PACK),
             )
 
@@ -132,9 +123,11 @@ def tile_list_laundry_dosing_scores_kernel(
         def picks(h):
             return offsets[:, (HALF // 16) * h : (HALF // 16) * (h + 1)]
 
-        def gather_words(a, h, tag):
+        def gather_words(a, h, tag, piece=HALF):
             v[a, h] = keep.tile([P, HALF], U32, name="v%d%d" % (a, h), tag=tag, align_bytes=64)
-            nc.vector.tensor_copy(v[a, h][:], tab[a][:].bitcast(U32).indirect(picks(h)))
+            for c0 in range(0, HALF, piece):
+                j0 = HALF * h + c0
+                nc.vector.tensor_copy(v[a, h][:, c0 : c0 + piece], tab[a][:].bitcast(U32).indirect(offsets[:, j0 // 16 : (j0 + piece) // 16]))
 
         def gather_scales(h, tag):
             v_sc[h] = keep.tile([P, HALF], U8, name="v_sc%d" % h, tag=tag, align_bytes=64)
@@ -161,6 +154,20 @@ def tile_list_laundry_dosing_scores_kernel(
             )
             return grouped
 
+        def quantize_w1_halves(a, b, engines):
+            codes = held("w1q%d%d" % (a, b), [P, PASS], U32)
+            scales = held("w1q%d%d_sc" % (a, b), [P, PASS], U8)
+            for e, engine in enumerate(engines):
+                grouped = work.tile([P, 2 * PASS], BF16, name="w1_half", bufs=4, align_bytes=64)
+                copy_on(
+                    engine,
+                    grouped[:].rearrange("p (t m i) -> p m i t", t=2, i=PACK),
+                    w1_raw[a, b][:].rearrange("p i (m t) -> p m i t", t=PACK)[:, :, :, 2 * e : 2 * e + 2],
+                )
+                cols = slice(256 * e, 256 * (e + 1))
+                nc.vector.quantize_mx(codes[:, cols].bitcast(E4M3), scales[:, cols], grouped[:])
+            return codes, scales
+
         def round_w3(b, engine):
             grouped = work.tile([P, PACK * PASS], BF16, name="w_grouped", align_bytes=64)
             copy_on(
@@ -173,27 +180,21 @@ def tile_list_laundry_dosing_scores_kernel(
         w1q = {}
         gather_words(0, 0, "v00")
         gather_scales(0, "v_sc0")
-        deal_wx_scales(0, "wx_sc0")
+        deal_wx_scales(0)
+        deal_wx_scales(1)
         w1q[0, 0] = quantize("w1q00", round_w1(0, 0, "scalar", "v_sc1"))
-        codes10 = held("w1q10", [P, PASS], U32)
-        scales10 = held("w1q10_sc", [P, PASS], U8)
-        for e in range(2):
-            grouped = keep.tile([P, 2 * PASS], BF16, name="w1_half%d" % e, tag=["w1_half0", "wx_sc1"][e], align_bytes=64)
-            nc.scalar.copy(
-                grouped[:].rearrange("p (t m i) -> p m i t", t=2, i=PACK),
-                w1_raw[1, 0][:].rearrange("p i (m t) -> p m i t", t=PACK)[:, :, :, 2 * e : 2 * e + 2],
-            )
-            cols = slice(256 * e, 256 * (e + 1))
-            nc.vector.quantize_mx(codes10[:, cols].bitcast(E4M3), scales10[:, cols], grouped[:])
-        w1q[1, 0] = codes10, scales10
-        gather_words(1, 0, "v10")
+        w1q[1, 0] = quantize_w1_halves(1, 0, ["scalar", "scalar"])
+        gather_words(1, 0, "v10", 256)
 
         gains = held("gains", [P, 2, 2, PACK], F32)
         nc.vector.tensor_copy(gains[:, :, 0, :], g1[:])
         nc.vector.tensor_scalar(gains[:, :, 1, :], g2[:], -1.0, None, ALU.mult)
 
-        def first_stage(b, h):
-            banks = [psum.tile([P, PACK, P], F32, name="bank") for c in range(PACK)]
+        def bank(k):
+            return psum.tile([P, PACK, P], F32, name="bank%d" % k)
+
+        def first_stage(b, h, chunks, bank_ids):
+            banks = {c: bank(k) for c, k in zip(chunks, bank_ids)}
 
             def table_pass(a, c):
                 codes, scales = w1q[a, b]
@@ -206,13 +207,13 @@ def tile_list_laundry_dosing_scores_kernel(
                         start=(a == 0 and t == 0), stop=(a == 1 and t == PACK - 1),
                     )
 
-            for c in range(PACK):
+            for c in chunks:
                 table_pass(0, c)
-            for c in range(PACK):
+            for c in chunks:
                 for t in range(PACK):
                     c0 = PASS * b + P * t
                     nc.tensor.matmul_mx(
-                        banks[c][:, t, :], lhsT=wx[:, 2 * c0 : 2 * (c0 + P)].bitcast(E2M1), lhsT_scale=wx_sc[b][:, P * t : P * (t + 1)],
+                        banks[c][:, t, :], lhsT=wx[:, 2 * c0 : 2 * (c0 + P)].bitcast(E2M1), lhsT_scale=wx_sc[:, c0 : c0 + P],
                         rhs=xs[h][:, P * c : P * (c + 1)].bitcast(E4M3), rhs_scale=xs_sc[:, HALF * h + P * c : HALF * h + P * (c + 1)],
                         start=False, stop=False,
                     )
@@ -225,34 +226,41 @@ def tile_list_laundry_dosing_scores_kernel(
         aq = {(b, h): operand("aq%d%d" % (b, h)) for b in range(2) for h in range(2)}
         bq = {(b, h): operand("bq%d%d" % (b, h)) for b in range(2) for h in range(2)}
 
-        def responses(b, h, banks, c0, width):
-            for d in range(c0, c0 + width, STEP):
-                step = min(STEP, width)
-                grouped = work.tile([P, 2, step // P, PASS], BF16, name="grouped", bufs=3, align_bytes=64)
-                for k in range(step // P):
-                    both = work.tile([P, 2, P, PACK], F32, name="both", bufs=5)
-                    sums = banks[d // P + k][:].rearrange("p t c -> p c t")
-                    nc.scalar.activation(both[:, 0], sums, ACT.Silu)
-                    nc.scalar.activation(both[:, 1], sums, ACT.Abs)
-                    nc.vector.tensor_tensor(
-                        grouped[:, :, k, :].rearrange("p e (c t) -> p e c t", t=PACK), both[:],
-                        gains[:, b].unsqueeze(2).broadcast_to([P, 2, P, PACK]), ALU.mult,
-                    )
-                cols = slice(d, d + step)
-                for e, (codes, scales) in enumerate((aq[b, h], bq[b, h])):
-                    nc.vector.quantize_mx(codes[:, cols].bitcast(E4M3), scales[:, cols], grouped[:, e].rearrange("p k c -> p (k c)"))
+        def scale(grouped, both, b, e0, e1):
+            nc.vector.tensor_tensor(
+                grouped.rearrange("p e (c t) -> p e c t", t=PACK), both[:, e0:e1],
+                gains[:, b, e0:e1].unsqueeze(2).broadcast_to([P, e1 - e0, P, PACK]), ALU.mult,
+            )
+
+        def responses(b, h, banks, first, count, apart=False):
+            grouped = work.tile([P, 2, count, PASS], BF16, name="grouped", bufs=3, align_bytes=64)
+            cols = slice(P * first, P * (first + count))
+
+            def quantize_response(e):
+                codes, scales = (aq[b, h], bq[b, h])[e]
+                nc.vector.quantize_mx(codes[:, cols].bitcast(E4M3), scales[:, cols], grouped[:, e].rearrange("p k c -> p (k c)"))
+
+            for k in range(count):
+                both = work.tile([P, 2, P, PACK], F32, name="both", bufs=5)
+                sums = banks[first + k][:].rearrange("p t c -> p c t")
+                nc.scalar.activation(both[:, 0], sums, ACT.Silu)
+                nc.scalar.activation(both[:, 1], sums, ACT.Abs)
+                if apart:
+                    scale(grouped[:, 0:1, k, :], both, b, 0, 1)
+                    quantize_response(0)
+                    scale(grouped[:, 1:2, k, :], both, b, 1, 2)
+                    quantize_response(1)
+                else:
+                    scale(grouped[:, :, k, :], both, b, 0, 2)
+            if not apart:
+                quantize_response(0)
+                quantize_response(1)
 
         w3q = {}
 
-        def open_sums(width):
-            per_bank = HALF // width
-            return [psum.tile([P, per_bank, width], F32, name="bank") for k in range(N // P // per_bank)]
-
-        def second_stage(sums, b, h, c0, width):
-            per_bank = HALF // width
-            narrow = HALF if width == HALF else P
+        def second_stage(sums, b, h, cols):
+            per_bank = N // P // len(sums)
             codes, scales = w3q[b]
-            cols = slice(c0, c0 + width)
             for u in range(N // P):
                 m = slice(P * u, P * (u + 1))
                 nc.tensor.matmul_mx(
@@ -261,52 +269,60 @@ def tile_list_laundry_dosing_scores_kernel(
                     start=(b == 0 and u % per_bank == 0), stop=False,
                 )
             for u in range(N // P):
-                for d in range(0, width, narrow):
-                    part = slice(c0 + d, c0 + d + narrow)
-                    nc.tensor.matmul_mx(
-                        sums[u // per_bank][:, u % per_bank, d : d + narrow],
-                        lhsT=w4[:, b, 2 * P * u : 2 * P * (u + 1)].bitcast(E2M1),
-                        lhsT_scale=w4_sc[:, b, P * u : P * (u + 1)],
-                        rhs=bq[b, h][0][:, part].bitcast(E4M3), rhs_scale=bq[b, h][1][:, part],
-                        start=False, stop=(b == 1 and u % per_bank == per_bank - 1 and d + narrow == width),
-                    )
+                nc.tensor.matmul_mx(
+                    sums[u // per_bank][:, u % per_bank, :],
+                    lhsT=w4[:, b, 2 * P * u : 2 * P * (u + 1)].bitcast(E2M1),
+                    lhsT_scale=w4_sc[:, b, P * u : P * (u + 1)],
+                    rhs=bq[b, h][0][:, cols].bitcast(E4M3), rhs_scale=bq[b, h][1][:, cols],
+                    start=False, stop=(b == 1 and u % per_bank == per_bank - 1),
+                )
 
-        def store(sums, j0, width, engines):
-            per_bank = HALF // width
-            for k, bank in enumerate(sums):
-                result = work.tile([P, per_bank, width], F32, name="result", bufs=8)
-                copy_on(engines[k], result[:], bank[:])
-                rows = out[P * per_bank * k : P * per_bank * (k + 1), j0 : j0 + width]
-                nc.sync.dma_start(rows.rearrange("(u p) c -> p u c", p=P), result[:])
+        def store(sums, u0, j0, engine):
+            per_bank, width = sums.shape[1], sums.shape[2]
+            result = work.tile([P, per_bank, width], F32, name="result", bufs=8)
+            copy_on(engine, result[:], sums[:])
+            rows = out[P * u0 : P * (u0 + per_bank), j0 : j0 + width]
+            nc.sync.dma_start(rows.rearrange("(u p) c -> p u c", p=P), result[:])
 
-        banks00 = first_stage(0, 0)
+        banks00 = first_stage(0, 0, [0, 1, 2, 3], [0, 1, 2, 3])
         gather_words(0, 1, "v01")
         gather_scales(1, "v_sc1")
         gather_words(1, 1, "v11")
-        banks01 = first_stage(0, 1)
-        responses(0, 0, banks00, 0, HALF)
-        deal_wx_words(1)
-        deal_wx_scales(1, "wx_sc1")
+        banks01 = first_stage(0, 1, [0, 1], [4, 5])
+        responses(0, 0, banks00, 0, 2)
         w1q[0, 1] = quantize("w1q01", round_w1(0, 1, "scalar", "w1_grouped01"))
-        w1q[1, 1] = quantize("w1q11", round_w1(1, 1, "vector", "w1_grouped11"))
-        banks10 = first_stage(1, 0)
-        responses(0, 1, banks01, 0, HALF)
+        responses(0, 0, banks00, 2, 2)
+        w1q[1, 1] = quantize_w1_halves(1, 1, ["vector", "vector"])
+        banks10 = first_stage(1, 0, [0, 1, 2, 3], [6, 7, 0, 1])
+        responses(0, 1, banks01, 0, 2)
+        banks01 = first_stage(0, 1, [2, 3], [2, 3])
+        responses(1, 0, banks10, 0, 2)
         w3q[0] = quantize("w3q0", round_w3(0, "scalar"))
-        sums0 = open_sums(HALF)
-        second_stage(sums0, 0, 0, 0, HALF)
-        responses(1, 0, banks10, 0, HALF)
-        banks11 = first_stage(1, 1)
+        sums0 = [psum.tile([P, 1, HALF], F32, name="bank%d" % (4 + u)) for u in range(N // P)]
+        second_stage(sums0, 0, 0, slice(0, HALF))
+        responses(1, 0, banks10, 2, 2)
         w3q[1] = quantize("w3q1", round_w3(1, "scalar"))
-        second_stage(sums0, 1, 0, 0, HALF)
-        chunks = [(0, 128), (128, 128), (256, 128), (384, 128)]
-        responses(1, 1, banks11, chunks[0][0], chunks[0][1])
-        store(sums0, 0, HALF, ["scalar"] * 4)
-        sums1 = [open_sums(width) for c0, width in chunks]
-        for sums, (c0, width) in zip(sums1, chunks):
-            second_stage(sums, 0, 1, c0, width)
-        for k, (c0, width) in enumerate(chunks):
-            if k > 0:
-                responses(1, 1, banks11, c0, width)
-                store(sums1[k - 1], HALF + chunks[k - 1][0], chunks[k - 1][1], ["scalar", "scalar"])
-            second_stage(sums1[k], 1, 1, c0, width)
-        store(sums1[-1], HALF + chunks[-1][0], chunks[-1][1], ["scalar", "vector"])
+        second_stage(sums0, 1, 0, slice(0, HALF))
+        banks11 = first_stage(1, 1, [0, 1], [0, 1])
+        responses(0, 1, banks01, 2, 2)
+        banks11.update(first_stage(1, 1, [2, 3], [2, 3]))
+        for u in [0]:
+            store(sums0[u], u, 0, (["scalar"] * 4)[u])
+        sums1 = []
+        for c in range(PACK):
+            cols = slice(P * c, P * (c + 1))
+            last = c == PACK - 1
+            responses(1, 1, banks11, c, 1, c >= 3)
+            for u in [[1], [2], [3], []][c]:
+                store(sums0[u], u, 0, (["scalar"] * 4)[u])
+            if last:
+                sums = [psum.tile([P, 2, P], F32, name="bank%d" % k) for k in (7, 0)]
+            else:
+                sums = [psum.tile([P, PACK, P], F32, name="bank%d" % (4 + c))]
+            second_stage(sums, 0, 1, cols)
+            second_stage(sums, 1, 1, cols)
+            sums1.append(sums)
+            if c >= 1:
+                store(sums1[c - 1][0], 0, HALF + P * (c - 1), (["scalar"] * 3)[c - 1])
+        store(sums1[-1][0], 0, HALF + P * (PACK - 1), "scalar")
+        store(sums1[-1][1], 2, HALF + P * (PACK - 1), "vector")

from contextlib import ExitStack

import concourse.mybir as mybir

K, K2, H, N, T, S = 1024, 512, 1024, 512, 2048, 1024
FLOPS = 2 * S * (K * H + K2 * H + 2 * H * N)

F32 = mybir.dt.float32
BF16 = mybir.dt.bfloat16
I32 = mybir.dt.int32
U32 = mybir.dt.uint32
U16 = mybir.dt.uint16
U8 = mybir.dt.uint8
E4M3 = mybir.dt.float8_e4m3fn_x4
E2M1 = mybir.dt.float4_e2m1fn_x4
ACT = mybir.ActivationFunctionType
ALU = mybir.AluOpType

P = 128
PACK = 4
PASS = P * PACK
HALF = 512
QUADS = 4
STEP = 256


def tile_list_laundry_dosing_scores_kernel(
    tc, tab_words, tab_scales, offs, w1, xs_words, xs_scales, wx_words, wx_scales,
    gain1, gain2, w3, w4_words, w4_scales, out,
):
    nc = tc.nc
    with ExitStack() as ctx:
        keep = ctx.enter_context(tc.tile_pool(name="keep", bufs=1))
        work = ctx.enter_context(tc.tile_pool(name="work", bufs=2))
        psum = ctx.enter_context(tc.psum_pool(name="psum", bufs=1))

        def held(name, shape, dtype):
            return keep.tile(shape, dtype, name=name, align_bytes=64)

        offsets = keep.tile([P, S // 16], U16, name="offsets")
        nc.sync.dma_start(offsets[:], offs)

        warm_in = held("warm_in", [P, 8], F32)
        warm_out = held("warm_out", [P, 8], F32)
        nc.vector.memset(warm_in[:], 0.0)
        nc.scalar.activation(warm_out[:], warm_in[:], ACT.Silu)

        tab_sc = held("tab_sc", [P, T], U8)
        wx_sc_raw = held("wx_sc_raw", [P, H], U8)
        xs_sc = held("xs_sc", [P, S], U8)
        w4_sc = held("w4_sc", [P, 2, N], U8)
        nc.gpsimd.memset(tab_sc[:].bitcast(I32), 0)
        nc.gpsimd.memset(wx_sc_raw[:].bitcast(I32), 0)
        nc.gpsimd.memset(xs_sc[:].bitcast(I32), 0)
        nc.gpsimd.memset(w4_sc[:].bitcast(I32), 0)

        wx_raw = held("wx_raw", [P, 2 * H], U8)
        xs = [held("xs%d" % h, [P, HALF], I32) for h in range(2)]

        def load_xs(h):
            nc.sync.dma_start(xs[h][:], xs_words[0].rearrange("p n i -> p (n i)").bitcast(I32)[:, HALF * h : HALF * (h + 1)])

        nc.sync.dma_start(wx_raw[:].bitcast(I32), wx_words[0].bitcast(I32))

        tab = [held("tab%d" % a, [P, T], I32) for a in range(2)]

        def load_tab(a):
            nc.sync.dma_start(tab[a][:], tab_words[a].rearrange("p n i -> p (n i)").bitcast(I32))

        def load_w(name, rows):
            raw = held(name, [P, PACK, rows.shape[1]], F32)
            nc.sync.dma_start(raw[:], rows.rearrange("(p i) c -> p i c", i=PACK))
            return raw

        def w1_rows(a, b):
            return w1[PASS * a : PASS * (a + 1), PASS * b : PASS * (b + 1)]

        load_tab(0)
        for q in range(QUADS):
            nc.sync.dma_start(tab_sc[32 * q : 32 * q + 8, :].bitcast(I32), tab_scales[:, 4 * q : 4 * q + 4, :].bitcast(I32))
        w1_raw = {}
        w1_raw[0, 0] = load_w("w1_raw00", w1_rows(0, 0))
        for q in range(QUADS):
            nc.sync.dma_start(wx_sc_raw[32 * q : 32 * q + 4, :].bitcast(I32), wx_scales[0, 4 * q : 4 * q + 4, :].bitcast(I32))
        w1_raw[1, 0] = load_w("w1_raw10", w1_rows(1, 0))
        load_tab(1)
        for q in range(QUADS):
            nc.sync.dma_start(xs_sc[32 * q : 32 * q + 4, :].bitcast(I32), xs_scales[0, 4 * q : 4 * q + 4, :].bitcast(I32))
        load_xs(0)
        g1 = held("g1", [P, 2, PACK], F32)
        g2 = held("g2", [P, 2, PACK], F32)
        nc.sync.dma_start(g1[:], gain1.rearrange("(b p t) -> p b t", b=2, t=PACK))
        nc.sync.dma_start(g2[:], gain2.rearrange("(b p t) -> p b t", b=2, t=PACK))
        load_xs(1)
        w1_raw[0, 1] = load_w("w1_raw01", w1_rows(0, 1))
        w1_raw[1, 1] = load_w("w1_raw11", w1_rows(1, 1))
        w3_raw = [load_w("w3_raw%d" % b, w3[PASS * b : PASS * (b + 1), :]) for b in range(2)]
        w4 = held("w4", [P, 2, 2 * N], U8)
        nc.sync.dma_start(w4[:].bitcast(I32), w4_words.rearrange("b p n -> p b n").bitcast(I32))
        for q in range(QUADS):
            nc.sync.dma_start(
                w4_sc[32 * q : 32 * q + 4, :, :].bitcast(I32),
                w4_scales[:, 4 * q : 4 * q + 4, :].rearrange("b r n -> r b n").bitcast(I32),
            )

        wx = held("wx", [P, 2 * H], U8)
        wx_sc = held("wx_sc", [P, H], U8)
        nc.vector.tensor_copy(
            wx[:].bitcast(U16).rearrange("p (b t m) -> p b m t", b=2, t=PACK),
            wx_raw[:].bitcast(U16).rearrange("p (b m t) -> p b m t", b=2, t=PACK),
        )

        def deal_wx_scales(b):
            cols = slice(PASS * b, PASS * (b + 1))
            nc.vector.tensor_copy(
                wx_sc[:, cols].rearrange("p (t m) -> p m t", t=PACK),
                wx_sc_raw[:, cols].rearrange("p (m t) -> p m t", t=PACK),
            )

        v = {}
        v_sc = {}

        def picks(h):
            return offsets[:, (HALF // 16) * h : (HALF // 16) * (h + 1)]

        def gather_words(a, h, tag, piece=HALF):
            v[a, h] = keep.tile([P, HALF], U32, name="v%d%d" % (a, h), tag=tag, align_bytes=64)
            for c0 in range(0, HALF, piece):
                j0 = HALF * h + c0
                nc.vector.tensor_copy(v[a, h][:, c0 : c0 + piece], tab[a][:].bitcast(U32).indirect(offsets[:, j0 // 16 : (j0 + piece) // 16]))

        def gather_scales(h, tag):
            v_sc[h] = keep.tile([P, HALF], U8, name="v_sc%d" % h, tag=tag, align_bytes=64)
            nc.vector.tensor_copy(v_sc[h][:], tab_sc[:].indirect(picks(h)))

        def copy_on(engine, dst, src):
            if engine == "scalar":
                nc.scalar.copy(dst, src)
            else:
                nc.vector.tensor_copy(dst, src)

        def quantize(name, grouped):
            codes = held(name, [P, PASS], U32)
            scales = held(name + "_sc", [P, PASS], U8)
            nc.vector.quantize_mx(codes[:].bitcast(E4M3), scales[:], grouped[:])
            return codes, scales

        def round_w1(a, b, engine, tag):
            grouped = keep.tile([P, PACK * PASS], BF16, name="w1_grouped%d%d" % (a, b), tag=tag, align_bytes=64)
            copy_on(
                engine,
                grouped[:].rearrange("p (t m i) -> p m i t", t=PACK, i=PACK),
                w1_raw[a, b][:].rearrange("p i (m t) -> p m i t", t=PACK),
            )
            return grouped

        def quantize_w1_halves(a, b, engines):
            codes = held("w1q%d%d" % (a, b), [P, PASS], U32)
            scales = held("w1q%d%d_sc" % (a, b), [P, PASS], U8)
            for e, engine in enumerate(engines):
                grouped = work.tile([P, 2 * PASS], BF16, name="w1_half", bufs=4, align_bytes=64)
                copy_on(
                    engine,
                    grouped[:].rearrange("p (t m i) -> p m i t", t=2, i=PACK),
                    w1_raw[a, b][:].rearrange("p i (m t) -> p m i t", t=PACK)[:, :, :, 2 * e : 2 * e + 2],
                )
                cols = slice(256 * e, 256 * (e + 1))
                nc.vector.quantize_mx(codes[:, cols].bitcast(E4M3), scales[:, cols], grouped[:])
            return codes, scales

        def round_w3(b, engine):
            grouped = work.tile([P, PACK * PASS], BF16, name="w_grouped", align_bytes=64)
            copy_on(
                engine,
                grouped[:].rearrange("p (c n i) -> p c i n", n=4, i=PACK),
                w3_raw[b][:].rearrange("p i (c n) -> p c i n", n=4),
            )
            return grouped

        w1q = {}
        gather_words(0, 0, "v00")
        gather_scales(0, "v_sc0")
        deal_wx_scales(0)
        deal_wx_scales(1)
        w1q[0, 0] = quantize("w1q00", round_w1(0, 0, "scalar", "v_sc1"))
        w1q[1, 0] = quantize_w1_halves(1, 0, ["scalar", "scalar"])
        gather_words(1, 0, "v10", 256)

        gains = held("gains", [P, 2, 2, PACK], F32)
        nc.vector.tensor_copy(gains[:, :, 0, :], g1[:])
        nc.vector.tensor_scalar(gains[:, :, 1, :], g2[:], -1.0, None, ALU.mult)

        def bank(k):
            return psum.tile([P, PACK, P], F32, name="bank%d" % k)

        def first_stage(b, h, chunks, bank_ids):
            banks = {c: bank(k) for c, k in zip(chunks, bank_ids)}

            def table_pass(a, c):
                codes, scales = w1q[a, b]
                cols = slice(P * c, P * (c + 1))
                for t in range(PACK):
                    m = slice(P * t, P * (t + 1))
                    nc.tensor.matmul_mx(
                        banks[c][:, t, :], lhsT=codes[:, m].bitcast(E4M3), lhsT_scale=scales[:, m],
                        rhs=v[a, h][:, cols].bitcast(E4M3), rhs_scale=v_sc[h][4 * a : P, cols],
                        start=(a == 0 and t == 0), stop=(a == 1 and t == PACK - 1),
                    )

            for c in chunks:
                table_pass(0, c)
            for c in chunks:
                for t in range(PACK):
                    c0 = PASS * b + P * t
                    nc.tensor.matmul_mx(
                        banks[c][:, t, :], lhsT=wx[:, 2 * c0 : 2 * (c0 + P)].bitcast(E2M1), lhsT_scale=wx_sc[:, c0 : c0 + P],
                        rhs=xs[h][:, P * c : P * (c + 1)].bitcast(E4M3), rhs_scale=xs_sc[:, HALF * h + P * c : HALF * h + P * (c + 1)],
                        start=False, stop=False,
                    )
                table_pass(1, c)
            return banks

        def operand(name):
            return held(name, [P, HALF], U32), held(name + "_sc", [P, HALF], U8)

        aq = {(b, h): operand("aq%d%d" % (b, h)) for b in range(2) for h in range(2)}
        bq = {(b, h): operand("bq%d%d" % (b, h)) for b in range(2) for h in range(2)}

        def scale(grouped, both, b, e0, e1):
            nc.vector.tensor_tensor(
                grouped.rearrange("p e (c t) -> p e c t", t=PACK), both[:, e0:e1],
                gains[:, b, e0:e1].unsqueeze(2).broadcast_to([P, e1 - e0, P, PACK]), ALU.mult,
            )

        def responses(b, h, banks, first, count, apart=False):
            grouped = work.tile([P, 2, count, PASS], BF16, name="grouped", bufs=3, align_bytes=64)
            cols = slice(P * first, P * (first + count))

            def quantize_response(e):
                codes, scales = (aq[b, h], bq[b, h])[e]
                nc.vector.quantize_mx(codes[:, cols].bitcast(E4M3), scales[:, cols], grouped[:, e].rearrange("p k c -> p (k c)"))

            for k in range(count):
                both = work.tile([P, 2, P, PACK], F32, name="both", bufs=5)
                sums = banks[first + k][:].rearrange("p t c -> p c t")
                nc.scalar.activation(both[:, 0], sums, ACT.Silu)
                nc.scalar.activation(both[:, 1], sums, ACT.Abs)
                if apart:
                    scale(grouped[:, 0:1, k, :], both, b, 0, 1)
                    quantize_response(0)
                    scale(grouped[:, 1:2, k, :], both, b, 1, 2)
                    quantize_response(1)
                else:
                    scale(grouped[:, :, k, :], both, b, 0, 2)
            if not apart:
                quantize_response(0)
                quantize_response(1)

        w3q = {}

        def second_stage(sums, b, h, cols):
            per_bank = N // P // len(sums)
            codes, scales = w3q[b]
            for u in range(N // P):
                m = slice(P * u, P * (u + 1))
                nc.tensor.matmul_mx(
                    sums[u // per_bank][:, u % per_bank, :], lhsT=codes[:, m].bitcast(E4M3), lhsT_scale=scales[:, m],
                    rhs=aq[b, h][0][:, cols].bitcast(E4M3), rhs_scale=aq[b, h][1][:, cols],
                    start=(b == 0 and u % per_bank == 0), stop=False,
                )
            for u in range(N // P):
                nc.tensor.matmul_mx(
                    sums[u // per_bank][:, u % per_bank, :],
                    lhsT=w4[:, b, 2 * P * u : 2 * P * (u + 1)].bitcast(E2M1),
                    lhsT_scale=w4_sc[:, b, P * u : P * (u + 1)],
                    rhs=bq[b, h][0][:, cols].bitcast(E4M3), rhs_scale=bq[b, h][1][:, cols],
                    start=False, stop=(b == 1 and u % per_bank == per_bank - 1),
                )

        def store(sums, u0, j0, engine):
            per_bank, width = sums.shape[1], sums.shape[2]
            result = work.tile([P, per_bank, width], F32, name="result", bufs=8)
            copy_on(engine, result[:], sums[:])
            rows = out[P * u0 : P * (u0 + per_bank), j0 : j0 + width]
            nc.sync.dma_start(rows.rearrange("(u p) c -> p u c", p=P), result[:])

        banks00 = first_stage(0, 0, [0, 1, 2, 3], [0, 1, 2, 3])
        gather_words(0, 1, "v01")
        gather_scales(1, "v_sc1")
        gather_words(1, 1, "v11")
        banks01 = first_stage(0, 1, [0, 1], [4, 5])
        responses(0, 0, banks00, 0, 2)
        w1q[0, 1] = quantize("w1q01", round_w1(0, 1, "scalar", "w1_grouped01"))
        responses(0, 0, banks00, 2, 2)
        w1q[1, 1] = quantize_w1_halves(1, 1, ["vector", "vector"])
        banks10 = first_stage(1, 0, [0, 1, 2, 3], [6, 7, 0, 1])
        responses(0, 1, banks01, 0, 2)
        banks01 = first_stage(0, 1, [2, 3], [2, 3])
        responses(1, 0, banks10, 0, 2)
        w3q[0] = quantize("w3q0", round_w3(0, "scalar"))
        sums0 = [psum.tile([P, 1, HALF], F32, name="bank%d" % (4 + u)) for u in range(N // P)]
        second_stage(sums0, 0, 0, slice(0, HALF))
        responses(1, 0, banks10, 2, 2)
        w3q[1] = quantize("w3q1", round_w3(1, "scalar"))
        second_stage(sums0, 1, 0, slice(0, HALF))
        banks11 = first_stage(1, 1, [0, 1], [0, 1])
        responses(0, 1, banks01, 2, 2)
        banks11.update(first_stage(1, 1, [2, 3], [2, 3]))
        for u in [0]:
            store(sums0[u], u, 0, (["scalar"] * 4)[u])
        sums1 = []
        for c in range(PACK):
            cols = slice(P * c, P * (c + 1))
            last = c == PACK - 1
            responses(1, 1, banks11, c, 1, c >= 3)
            for u in [[1], [2], [3], []][c]:
                store(sums0[u], u, 0, (["scalar"] * 4)[u])
            if last:
                sums = [psum.tile([P, 2, P], F32, name="bank%d" % k) for k in (7, 0)]
            else:
                sums = [psum.tile([P, PACK, P], F32, name="bank%d" % (4 + c))]
            second_stage(sums, 0, 1, cols)
            second_stage(sums, 1, 1, cols)
            sums1.append(sums)
            if c >= 1:
                store(sums1[c - 1][0], 0, HALF + P * (c - 1), (["scalar"] * 3)[c - 1])
        store(sums1[-1][0], 0, HALF + P * (PACK - 1), "scalar")
        store(sums1[-1][1], 2, HALF + P * (PACK - 1), "vector")
